import numpy as np
import ml_dtypes

BF16 = ml_dtypes.bfloat16


def bf(x):
    return np.asarray(x, np.float32).astype(BF16)


def f32(x):
    return np.asarray(x, np.float32)


def f64(x):
    return np.asarray(x).astype(np.float64)


def striped(idx):
    return np.tile(idx.reshape(-1, 16).T, (8, 1))


S, K, M, N, D, V = 512, 128, 256, 768, 16, 48


def gelu_tanh(v):
    return 0.5 * v * (1.0 + np.tanh(np.sqrt(2.0 / np.pi) * (v + 0.044715 * v**3)))


def setup_inputs():
    return {"table": bf(np.random.standard_normal((K, S))), "w": bf(np.random.standard_normal((K, M)) / np.sqrt(K)), "b": f32(0.5 * np.random.standard_normal((M, 1))), "offs": striped(np.random.permutation(np.tile(np.arange(S), 2))[:N])}


def reference(table, w, b, offs):
    idx = offs[:16].T.reshape(-1)
    x = f64(table)[:, idx]
    y = f64(w).T @ x
    z = gelu_tanh(y + f64(b))
    return z.reshape(M, V, D).max(axis=2)

@@ -1,0 +1,59 @@
+import concourse.mybir as mybir
+
+BF16, F32, U16 = mybir.dt.bfloat16, mybir.dt.float32, mybir.dt.uint16
+
+P = 128
+S = 512
+M = 256
+N = 768
+D = 16
+PER_COLUMN = 16
+
+PIECE = 128
+PSUM_BANKS = 8
+PIECE_COLUMNS = PIECE // PER_COLUMN
+PIECE_NODES = PIECE // D
+
+FLOPS = 2 * P * M * N
+
+
+def tile_gather_matmul_kernel(tc, table, w, b, offs, out):
+    nc = tc.nc
+    gelu = mybir.ActivationFunctionType.Gelu_apprx_tanh
+    blocks = M // P
+    pieces = N // PIECE
+    with (
+        tc.tile_pool(name="held", bufs=1) as held,
+        tc.tile_pool(name="work", bufs=blocks * pieces) as work,
+        tc.tile_pool(name="result", bufs=blocks) as result,
+        tc.psum_pool(name="psum", bufs=min(blocks * pieces, PSUM_BANKS)) as psum,
+    ):
+        nodes = held.tile([P, S], BF16, name="nodes")
+        nc.sync.dma_start(nodes[:], table)
+        weights = held.tile([P, M], BF16, name="weights")
+        nc.scalar.dma_start(weights[:], w)
+        offsets = held.tile([P, N // PER_COLUMN], U16, name="offsets")
+        nc.sync.dma_start(offsets[:], offs)
+        bias = held.tile([P, blocks], F32, name="bias")
+        nc.scalar.dma_start(bias[:], b.rearrange("(a p) o -> p (a o)", p=P))
+
+        zeros = held.tile([P, 1], F32, name="zeros")
+        nc.vector.memset(zeros[:], 0.0)
+        unused = held.tile([P, 1], F32, name="unused")
+        nc.scalar.activation(unused[:], zeros[:], gelu)
+
+        for a in range(blocks):
+            pooled = result.tile([P, N // D], F32, name="pooled")
+            for q in range(pieces):
+                picked = nodes[:].indirect(offsets[:, q * PIECE_COLUMNS : (q + 1) * PIECE_COLUMNS])
+                product = psum.tile([P, PIECE], F32, name="product")
+                nc.tensor.matmul(product[:], weights[:, a * P : (a + 1) * P], picked, start=True, stop=True)
+                z = work.tile([P, PIECE], F32, name="z")
+                nc.scalar.activation(z[:], product[:], gelu, bias=bias[:, a : a + 1])
+                nc.vector.tensor_reduce(
+                    pooled[:, q * PIECE_NODES : (q + 1) * PIECE_NODES],
+                    z[:].rearrange("p (v t) -> p v t", t=D),
+                    axis=mybir.AxisListType.X,
+                    op=mybir.AluOpType.max,
+                )
+            nc.sync.dma_start(out[a * P : (a + 1) * P, :], pooled[:])

@@ -35,7 +35,7 @@ def tile_gather_matmul_kernel(tc, table, w, b, offs, out):
         offsets = held.tile([P, N // PER_COLUMN], U16, name="offsets")
         nc.sync.dma_start(offsets[:], offs)
         bias = held.tile([P, blocks], F32, name="bias")
-        nc.scalar.dma_start(bias[:], b.rearrange("(a p) o -> p (a o)", p=P))
+        nc.scalar.dma_start(bias[:], b.rearrange("(p a) o -> p (a o)", a=blocks))
 
         zeros = held.tile([P, 1], F32, name="zeros")
         nc.vector.memset(zeros[:], 0.0)
@@ -47,7 +47,7 @@ def tile_gather_matmul_kernel(tc, table, w, b, offs, out):
             for q in range(pieces):
                 picked = nodes[:].indirect(offsets[:, q * PIECE_COLUMNS : (q + 1) * PIECE_COLUMNS])
                 product = psum.tile([P, PIECE], F32, name="product")
-                nc.tensor.matmul(product[:], weights[:, a * P : (a + 1) * P], picked, start=True, stop=True)
+                nc.tensor.matmul(product[:], weights[:, a::blocks], picked, start=True, stop=True)
                 z = work.tile([P, PIECE], F32, name="z")
                 nc.scalar.activation(z[:], product[:], gelu, bias=bias[:, a : a + 1])
                 nc.vector.tensor_reduce(
@@ -56,4 +56,4 @@ def tile_gather_matmul_kernel(tc, table, w, b, offs, out):
                     axis=mybir.AxisListType.X,
                     op=mybir.AluOpType.max,
                 )
-            nc.sync.dma_start(out[a * P : (a + 1) * P, :], pooled[:])
+            nc.sync.dma_start(out.rearrange("(p a) v -> p a v", a=blocks)[:, a, :], pooled[:])

@@ -14,6 +14,8 @@ PSUM_BANKS = 8
 PIECE_COLUMNS = PIECE // PER_COLUMN
 PIECE_NODES = PIECE // D
 
+LATE_PIECES = 2
+
 FLOPS = 2 * P * M * N
 
 
@@ -25,7 +27,7 @@ def tile_gather_matmul_kernel(tc, table, w, b, offs, out):
     with (
         tc.tile_pool(name="held", bufs=1) as held,
         tc.tile_pool(name="work", bufs=blocks * pieces) as work,
-        tc.tile_pool(name="result", bufs=blocks) as result,
+        tc.tile_pool(name="result", bufs=1) as result,
         tc.psum_pool(name="psum", bufs=min(blocks * pieces, PSUM_BANKS)) as psum,
     ):
         nodes = held.tile([P, S], BF16, name="nodes")
@@ -42,18 +44,25 @@ def tile_gather_matmul_kernel(tc, table, w, b, offs, out):
         unused = held.tile([P, 1], F32, name="unused")
         nc.scalar.activation(unused[:], zeros[:], gelu)
 
+        out_runs = out.rearrange("(p a) v -> p (a v)", a=blocks)
+        late_nodes = LATE_PIECES * PIECE_NODES
+        early_nodes = blocks * pieces * PIECE_NODES - late_nodes
+        early = result.tile([P, early_nodes], F32, name="early")
+        late = result.tile([P, late_nodes], F32, name="late")
         for a in range(blocks):
-            pooled = result.tile([P, N // D], F32, name="pooled")
             for q in range(pieces):
                 picked = nodes[:].indirect(offsets[:, q * PIECE_COLUMNS : (q + 1) * PIECE_COLUMNS])
                 product = psum.tile([P, PIECE], F32, name="product")
                 nc.tensor.matmul(product[:], weights[:, a::blocks], picked, start=True, stop=True)
                 z = work.tile([P, PIECE], F32, name="z")
                 nc.scalar.activation(z[:], product[:], gelu, bias=bias[:, a : a + 1])
+                node = (a * pieces + q) * PIECE_NODES
+                pooled, first = (early, node) if node < early_nodes else (late, node - early_nodes)
                 nc.vector.tensor_reduce(
-                    pooled[:, q * PIECE_NODES : (q + 1) * PIECE_NODES],
+                    pooled[:, first : first + PIECE_NODES],
                     z[:].rearrange("p (v t) -> p v t", t=D),
                     axis=mybir.AxisListType.X,
                     op=mybir.AluOpType.max,
                 )
-            nc.sync.dma_start(out.rearrange("(p a) v -> p a v", a=blocks)[:, a, :], pooled[:])
+        nc.sync.dma_start(out_runs[:, :early_nodes], early[:])
+        nc.sync.dma_start(out_runs[:, early_nodes:], late[:])

import concourse.mybir as mybir

BF16, F32, U16 = mybir.dt.bfloat16, mybir.dt.float32, mybir.dt.uint16

P = 128
S = 512
M = 256
N = 768
D = 16
PER_COLUMN = 16

PIECE = 128
PSUM_BANKS = 8
PIECE_COLUMNS = PIECE // PER_COLUMN
PIECE_NODES = PIECE // D

LATE_PIECES = 2

FLOPS = 2 * P * M * N


def tile_gather_matmul_kernel(tc, table, w, b, offs, out):
    nc = tc.nc
    gelu = mybir.ActivationFunctionType.Gelu_apprx_tanh
    blocks = M // P
    pieces = N // PIECE
    with (
        tc.tile_pool(name="held", bufs=1) as held,
        tc.tile_pool(name="work", bufs=blocks * pieces) as work,
        tc.tile_pool(name="result", bufs=1) as result,
        tc.psum_pool(name="psum", bufs=min(blocks * pieces, PSUM_BANKS)) as psum,
    ):
        nodes = held.tile([P, S], BF16, name="nodes")
        nc.sync.dma_start(nodes[:], table)
        weights = held.tile([P, M], BF16, name="weights")
        nc.scalar.dma_start(weights[:], w)
        offsets = held.tile([P, N // PER_COLUMN], U16, name="offsets")
        nc.sync.dma_start(offsets[:], offs)
        bias = held.tile([P, blocks], F32, name="bias")
        nc.scalar.dma_start(bias[:], b.rearrange("(p a) o -> p (a o)", a=blocks))

        zeros = held.tile([P, 1], F32, name="zeros")
        nc.vector.memset(zeros[:], 0.0)
        unused = held.tile([P, 1], F32, name="unused")
        nc.scalar.activation(unused[:], zeros[:], gelu)

        out_runs = out.rearrange("(p a) v -> p (a v)", a=blocks)
        late_nodes = LATE_PIECES * PIECE_NODES
        early_nodes = blocks * pieces * PIECE_NODES - late_nodes
        early = result.tile([P, early_nodes], F32, name="early")
        late = result.tile([P, late_nodes], F32, name="late")
        for a in range(blocks):
            for q in range(pieces):
                picked = nodes[:].indirect(offsets[:, q * PIECE_COLUMNS : (q + 1) * PIECE_COLUMNS])
                product = psum.tile([P, PIECE], F32, name="product")
                nc.tensor.matmul(product[:], weights[:, a::blocks], picked, start=True, stop=True)
                z = work.tile([P, PIECE], F32, name="z")
                nc.scalar.activation(z[:], product[:], gelu, bias=bias[:, a : a + 1])
                node = (a * pieces + q) * PIECE_NODES
                pooled, first = (early, node) if node < early_nodes else (late, node - early_nodes)
                nc.vector.tensor_reduce(
                    pooled[:, first : first + PIECE_NODES],
                    z[:].rearrange("p (v t) -> p v t", t=D),
                    axis=mybir.AxisListType.X,
                    op=mybir.AluOpType.max,
                )
        nc.sync.dma_start(out_runs[:, :early_nodes], early[:])
        nc.sync.dma_start(out_runs[:, early_nodes:], late[:])
